import numpy as np
import ml_dtypes


def mxq(x, axis, fmt="e4m3"):
    dtype, down = {"e4m3": (ml_dtypes.float8_e4m3fn, 7), "e5m2": (ml_dtypes.float8_e5m2, 14)}[fmt]
    v = np.moveaxis(np.asarray(x, np.float32).astype(ml_dtypes.bfloat16).astype(np.float64), axis, -1)
    blocks = v.reshape(v.shape[:-1] + (-1, 32))
    amax = np.abs(blocks).max(-1, keepdims=True)
    byte = np.maximum(np.where(amax > 0, np.frexp(amax)[1] - 1 + 127, 0) - down, 1)
    scale = np.exp2(byte - 127.0)
    codes = (blocks / scale).astype(np.float32).astype(dtype).astype(np.float64)
    return np.moveaxis((codes * scale).reshape(v.shape), -1, axis)


WIDE = False


def mx_kscale(k):
    if not WIDE:
        return np.ones(k)
    levels = np.array([10, -10, 5, -5, 0])
    if k % 512:
        return np.exp2(np.random.permutation(np.resize(levels, k // 32))).repeat(32)
    a = np.empty((k // 512, 16))
    for p in range(k // 512):
        a[p, :8] = np.random.permutation(np.resize(levels, 8))
        for g in range(8):
            far = levels[np.abs(levels - a[p, g]) >= 10]
            a[p, g + 8] = far[np.random.randint(len(far))]
    return np.exp2(a.ravel()).repeat(32)


def f64(x):
    return np.asarray(x).astype(np.float64)


def striped(idx):
    return np.tile(idx.reshape(-1, 16).T, (8, 1)).astype(np.uint16)


def unstriped(offs):
    return offs[:16].T.reshape(-1).astype(np.int64)


def pack_weight(w):
    k, n = w.shape
    w = f64(np.asarray(w, np.float32).astype(ml_dtypes.bfloat16)).reshape(k // 32, 32, n)
    amax = np.abs(w).max(1)
    byte = np.clip(np.where(amax > 0, np.frexp(amax)[1] - 1 + 127 - 7, 1), 1, 254)
    scaled = (w * np.exp2(127.0 - byte)[:, None, :]).reshape(k, n).astype(np.float32)
    words = np.ascontiguousarray(scaled.reshape(k // 512, 128, 4, n).transpose(0, 1, 3, 2)).astype(ml_dtypes.float8_e4m3fn).view(np.uint8)
    return words, np.ascontiguousarray(byte.astype(np.uint8).reshape(k // 512, 16, n))


def unpack_weight(words, scales):
    g, p, n, _ = words.shape
    vals = np.ascontiguousarray(words).view(ml_dtypes.float8_e4m3fn).astype(np.float64) * np.repeat(np.exp2(scales.astype(np.float64) - 127.0), 8, axis=1)[..., None]
    return vals.transpose(0, 1, 3, 2).reshape(g * 512, n)


def sigmoid(v):
    return 1.0 / (1.0 + np.exp(-np.maximum(v, -700.0)))


K, T, S, H, W = 512, 2048, 512, 512, 256


def setup_inputs():
    n = np.random.standard_normal
    s = mx_kscale(K)[:, None]
    u = mx_kscale(S)
    packed_xT = pack_weight(n((K, T)) * s)
    perm = np.random.permutation(H)
    return {
        "x_words": packed_xT[0],
        "x_scales": packed_xT[1],
        "wa": (n((K, H)) / np.sqrt(K) / s).astype(np.float32),
        "wb": (n((K, H)) / np.sqrt(K) / s).astype(np.float32),
        "gt": (np.random.uniform(0.5, 1.5, (S, 1)) * u[:, None]).astype(np.float32),
        "gi": (np.random.uniform(0.5, 1.5, (S, 1)) / u[:, None]).astype(np.float32),
        "offs": striped(np.random.permutation(T)[:S]),
        "two": striped(np.random.permutation(T)[:S]),
        "n1": striped(np.random.permutation(H)),
        "n2": striped(np.random.permutation(H)),
        "n3": striped(perm[:W]),
        "n4": striped(perm[W:]),
    }


def reference(x_words, x_scales, wa, wb, gt, gi, offs, two, n1, n2, n3, n4):
    xq = unpack_weight(x_words, x_scales)[:, unstriped(offs)]
    a = xq.T @ mxq(f64(wa), 0, "e4m3")
    x_two = unpack_weight(x_words, x_scales)[:, unstriped(two)]
    b = x_two.T @ mxq(f64(wb), 0, "e4m3")
    z = f64(gt) * (a * (sigmoid(b[:, unstriped(n2)])) - (0.5 * a[:, unstriped(n1)]))
    z2 = f64(gi) * b
    cv = 0.0625 * ((mxq(z, 0, "e4m3").T @ mxq(z2, 0, "e4m3")))
    pa = cv[:, unstriped(n3)]
    pb = cv[:, unstriped(n4)]
    ra = pa * sigmoid(pb)
    out = cv.copy()
    out[:, unstriped(n4)] = ra
    return out

@@ -1,0 +1,181 @@
+from contextlib import ExitStack
+
+import concourse.mybir as mybir
+
+K, T, S, H, W = 512, 2048, 512, 512, 256
+FLOPS = 3 * 2 * 512 * 512 * 512
+
+F32 = mybir.dt.float32
+BF16 = mybir.dt.bfloat16
+U32 = mybir.dt.uint32
+I32 = mybir.dt.int32
+U16 = mybir.dt.uint16
+U8 = mybir.dt.uint8
+FP8X4 = mybir.dt.float8_e4m3fn_x4
+ACT = mybir.ActivationFunctionType
+ALU = mybir.AluOpType
+
+P = 128
+PACK = 4
+BLK = 128
+NBLK = H // BLK
+HALF = H // 2
+
+
+def tile_picked_momtgatebfold_none_p_kernel(tc, x_words, x_scales, wa, wb, gt, gi, offs, two, n1, n2, n3, n4, out):
+    nc = tc.nc
+    with ExitStack() as ctx:
+        keep = ctx.enter_context(tc.tile_pool(name="keep", bufs=1))
+        psum = ctx.enter_context(tc.psum_pool(name="psum", bufs=1))
+
+        def sb(shape, dtype, name):
+            return keep.tile(shape, dtype, name=name, align_bytes=64)
+
+        def load_list(src, name):
+            dst = keep.tile(list(src.shape), U16, name=name)
+            nc.sync.dma_start(dst[:], src)
+            return dst
+
+        def entries(lst, first, count):
+            return lst[:, first // 16 : (first + count) // 16]
+
+        def weave_out(ap):
+            return ap.rearrange("p (c i) t -> p c t i", i=4)
+
+        def weave_in(ap):
+            return ap.rearrange("p t (c i) -> p c t i", i=4)
+
+        def quantize(codes, scales, woven):
+            nc.vector.quantize_mx(out=codes.bitcast(FP8X4), scales=scales, in_=woven.rearrange("p c t -> p (c t)"))
+
+        def product(acc, l_codes, l_scales, r_codes, r_scales):
+            nc.tensor.matmul_mx(out=acc, lhsT=l_codes.bitcast(FP8X4), lhsT_scale=l_scales,
+                                rhs=r_codes.bitcast(FP8X4), rhs_scale=r_scales, start=True, stop=True)
+
+        xs = sb([P, T], U8, "xs")
+        nc.vector.memset(xs[:].bitcast(I32), 0)
+        two_l = load_list(two, "two_l")
+        offs_l = load_list(offs, "offs_l")
+        gi_c = sb([P, PACK], F32, "gi_c")
+        nc.sync.dma_start(gi_c[:], gi.rearrange("(p t) o -> p (t o)", t=PACK))
+        gt_c = sb([P, PACK], F32, "gt_c")
+        nc.sync.dma_start(gt_c[:], gt.rearrange("(p t) o -> p (t o)", t=PACK))
+        n2_l = load_list(n2, "n2_l")
+        wb_raw = sb([P, PACK, H], F32, "wb_raw")
+        nc.sync.dma_start(wb_raw[:], wb.rearrange("(p j) c -> p j c", j=PACK))
+        n1_l = load_list(n1, "n1_l")
+        n3_l = load_list(n3, "n3_l")
+        for q in range(4):
+            nc.sync.dma_start(xs[32 * q : 32 * q + 4, :].bitcast(I32), x_scales[0, 4 * q : 4 * q + 4, :].bitcast(I32))
+        xw = sb([P, T], U32, "xw")
+        nc.sync.dma_start(xw[:].bitcast(I32), x_words[0].rearrange("p n t -> p (n t)").bitcast(I32))
+        wa_raw = sb([P, PACK, H], F32, "wa_raw")
+        nc.sync.dma_start(wa_raw[:], wa.rearrange("(p j) c -> p j c", j=PACK))
+        n4_l = load_list(n4, "n4_l")
+
+        def pick(window, lst, dtype, name, tag):
+            dst = keep.tile([P, S], dtype, name=name, tag=tag, align_bytes=64)
+            nc.vector.tensor_copy(dst[:].rearrange("p (t m) -> p m t", t=PACK), window[:].indirect(lst[:]))
+            return dst
+
+        wb_woven = sb([P, H, PACK], BF16, "wb_woven")
+        wb_q = sb([P, H], U32, "wb_q")
+        wb_s = sb([P, H], U8, "wb_s")
+        nc.scalar.copy(weave_out(wb_woven[:, :HALF, :]), weave_in(wb_raw[:, :, :HALF]))
+        nc.scalar.copy(weave_out(wb_woven[:, HALF:, :]), weave_in(wb_raw[:, :, HALF:]))
+        xb_s = pick(xs, two_l, U8, "xb_s", "xb_s")
+        quantize(wb_q[:, :HALF], wb_s[:, :HALF], wb_woven[:, :HALF, :])
+        xb_w = pick(xw, two_l, U32, "xb_w", "xb_w")
+        quantize(wb_q[:, HALF:], wb_s[:, HALF:], wb_woven[:, HALF:, :])
+        xa_s = pick(xs, offs_l, U8, "xa_s", "xa_s")
+        xa_w = pick(xw, offs_l, U32, "xa_w", "xa_w")
+
+        sig_b = sb([P, PACK, H], F32, "sig_b")
+        b_bank = []
+        for c in range(NBLK):
+            bank = psum.tile([P, PACK, BLK], F32, name=f"b_bank{c}", tag=f"left{c}")
+            cols = slice(c * BLK, (c + 1) * BLK)
+            for t in range(PACK):
+                toks = slice(t * P, (t + 1) * P)
+                product(bank[:, t, :], xb_w[:, toks], xb_s[:, toks], wb_q[:, cols], wb_s[:, cols])
+            nc.scalar.activation(sig_b[:, :, c * BLK : (c + 1) * BLK], bank[:], ACT.Sigmoid)
+            b_bank.append(bank)
+
+        wa_woven = sb([P, H, PACK], BF16, "wa_woven")
+        wa_q = sb([P, H], U32, "wa_q")
+        wa_s = sb([P, H], U8, "wa_s")
+        nc.vector.tensor_copy(weave_out(wa_woven[:]), weave_in(wa_raw[:]))
+        z2_woven = sb([P, H, PACK], BF16, "z2_woven")
+        gi_b = gi_c[:].unsqueeze(1).to_broadcast([P, BLK, PACK])
+
+        def make_z2(c):
+            nc.vector.tensor_tensor(z2_woven[:, c * BLK : (c + 1) * BLK, :], b_bank[c][:].rearrange("p t c -> p c t"), gi_b, ALU.mult)
+
+        quantize(wa_q[:], wa_s[:], wa_woven[:])
+
+        gate = sb([P, PACK, H], F32, "gate")
+        for h in range(2):
+            for t in range(PACK):
+                nc.scalar.activation(gate[:, t, h * HALF : (h + 1) * HALF], sig_b[:, t, :].indirect(entries(n2_l, h * HALF, HALF)), ACT.Copy)
+
+        half_a = sb([P, PACK, H], F32, "half_a")
+        half_gt = sb([P, PACK], F32, "half_gt")
+        nc.vector.tensor_scalar(half_gt[:], gt_c[:], 0.5, None, ALU.mult)
+        for c in range(NBLK):
+            bank = psum.tile([P, PACK, BLK], F32, name=f"a_bank{c}", tag=f"right{c}")
+            cols = slice(c * BLK, (c + 1) * BLK)
+            for t in range(PACK):
+                toks = slice(t * P, (t + 1) * P)
+                product(bank[:, t, :], xa_w[:, toks], xa_s[:, toks], wa_q[:, cols], wa_s[:, cols])
+            nc.vector.tensor_tensor(half_a[:, :, cols], bank[:], half_gt[:].unsqueeze(2).to_broadcast([P, PACK, BLK]), ALU.mult)
+        for c in range(NBLK):
+            make_z2(c)
+        z2_q = sb([P, H], U32, "z2_q")
+        z2_s = sb([P, H], U8, "z2_s")
+
+        looked = [sb([P, PACK, BLK], F32, f"looked{c}") for c in range(NBLK)]
+        for c in range(NBLK):
+            for t in range(PACK):
+                nc.scalar.activation(looked[c][:, t, :], half_a[:, t, :].indirect(entries(n1_l, c * BLK, BLK)), ACT.Copy)
+
+        cv = []
+
+        def make_cv(c):
+            cols = slice(c * BLK, (c + 1) * BLK)
+            gated = sb([P, PACK, BLK], F32, f"gated{c}")
+            nc.vector.scalar_tensor_tensor(gated[:], half_a[:, :, cols], 2.0, gate[:, :, cols], ALU.mult, ALU.mult)
+            if c == 0:
+                quantize(z2_q[:], z2_s[:], z2_woven[:])
+            z_woven = sb([P, BLK, PACK], BF16, f"z_woven{c}")
+            nc.vector.tensor_tensor(weave_out(z_woven[:]), weave_in(gated[:]), weave_in(looked[c][:]), ALU.subtract)
+            z_q = sb([P, BLK], U32, f"z_q{c}")
+            z_s = sb([P, BLK], U8, f"z_s{c}")
+            quantize(z_q[:], z_s[:], z_woven[:])
+            bank = psum.tile([P, H], F32, name=f"cv_bank{c}", tag=f"left{c}")
+            product(bank[:], z_q[:], z_s[:], z2_q[:], z2_s[:])
+            rows = sb([P, H], F32, f"cv{c}")
+            nc.vector.tensor_scalar(rows[:], bank[:], 0.0625, None, ALU.mult)
+            cv.append(rows)
+
+        ra = []
+
+        def fetch(c):
+            pa = sb([P, W], F32, f"pa{c}")
+            pb = sb([P, W], F32, f"pb{c}")
+            nc.scalar.activation(pa[:], cv[c][:].indirect(n3_l[:]), ACT.Copy)
+            nc.scalar.activation(pb[:], cv[c][:].indirect(n4_l[:]), ACT.Sigmoid)
+            r = sb([P, W], F32, f"ra{c}")
+            nc.vector.tensor_tensor(r[:], pa[:], pb[:], ALU.mult)
+            ra.append(r)
+
+        def put(c):
+            nc.scalar.activation(cv[c][:].indirect(n4_l[:]), ra[c][:], ACT.Copy)
+            nc.sync.dma_start(out[c * BLK : (c + 1) * BLK, :], cv[c][:])
+
+        for c in range(NBLK):
+            make_cv(c)
+        for c in range(NBLK):
+            fetch(c)
+            if c > 0:
+                put(c - 1)
+        put(NBLK - 1)

@@ -2,7 +2,7 @@ from contextlib import ExitStack
 
 import concourse.mybir as mybir
 
-K, T, S, H, W = 512, 2048, 512, 512, 256
+T, S, H, W = 2048, 512, 512, 256
 FLOPS = 3 * 2 * 512 * 512 * 512
 
 F32 = mybir.dt.float32
@@ -20,6 +20,8 @@ PACK = 4
 BLK = 128
 NBLK = H // BLK
 HALF = H // 2
+LINE = 4
+GPSIMD_BLOCKS = NBLK - 1
 
 
 def tile_picked_momtgatebfold_none_p_kernel(tc, x_words, x_scales, wa, wb, gt, gi, offs, two, n1, n2, n3, n4, out):
@@ -28,22 +30,24 @@ def tile_picked_momtgatebfold_none_p_kernel(tc, x_words, x_scales, wa, wb, gt, g
         keep = ctx.enter_context(tc.tile_pool(name="keep", bufs=1))
         psum = ctx.enter_context(tc.psum_pool(name="psum", bufs=1))
 
-        def sb(shape, dtype, name):
-            return keep.tile(shape, dtype, name=name, align_bytes=64)
+        def sb(shape, dtype, name, buffer=""):
+            return keep.tile(shape, dtype, name=name, tag=buffer, align_bytes=64)
 
         def load_list(src, name):
             dst = keep.tile(list(src.shape), U16, name=name)
             nc.sync.dma_start(dst[:], src)
             return dst
 
-        def entries(lst, first, count):
-            return lst[:, first // 16 : (first + count) // 16]
+        def load_by_place(src, name):
+            dst = sb([P, PACK], F32, name)
+            nc.sync.dma_start(dst[:], src.rearrange("(p t) o -> p (t o)", t=PACK))
+            return dst
 
-        def weave_out(ap):
-            return ap.rearrange("p (c i) t -> p c t i", i=4)
+        def weave_out(woven):
+            return woven.rearrange("p (c i) t -> p c t i", i=LINE)
 
-        def weave_in(ap):
-            return ap.rearrange("p t (c i) -> p c t i", i=4)
+        def weave_in(rows):
+            return rows.rearrange("p t (c i) -> p c t i", i=LINE)
 
         def quantize(codes, scales, woven):
             nc.vector.quantize_mx(out=codes.bitcast(FP8X4), scales=scales, in_=woven.rearrange("p c t -> p (c t)"))
@@ -52,103 +56,112 @@ def tile_picked_momtgatebfold_none_p_kernel(tc, x_words, x_scales, wa, wb, gt, g
             nc.tensor.matmul_mx(out=acc, lhsT=l_codes.bitcast(FP8X4), lhsT_scale=l_scales,
                                 rhs=r_codes.bitcast(FP8X4), rhs_scale=r_scales, start=True, stop=True)
 
+        blocks = [slice(c * BLK, (c + 1) * BLK) for c in range(NBLK)]
+        halves = [slice(h * HALF, (h + 1) * HALF) for h in range(2)]
+
+        def in_half(tiles, c):
+            return tiles[c // 2][:, :, blocks[c % 2]]
+
         xs = sb([P, T], U8, "xs")
         nc.vector.memset(xs[:].bitcast(I32), 0)
         two_l = load_list(two, "two_l")
         offs_l = load_list(offs, "offs_l")
-        gi_c = sb([P, PACK], F32, "gi_c")
-        nc.sync.dma_start(gi_c[:], gi.rearrange("(p t) o -> p (t o)", t=PACK))
-        gt_c = sb([P, PACK], F32, "gt_c")
-        nc.sync.dma_start(gt_c[:], gt.rearrange("(p t) o -> p (t o)", t=PACK))
-        n2_l = load_list(n2, "n2_l")
-        wb_raw = sb([P, PACK, H], F32, "wb_raw")
-        nc.sync.dma_start(wb_raw[:], wb.rearrange("(p j) c -> p j c", j=PACK))
-        n1_l = load_list(n1, "n1_l")
-        n3_l = load_list(n3, "n3_l")
-        for q in range(4):
-            nc.sync.dma_start(xs[32 * q : 32 * q + 4, :].bitcast(I32), x_scales[0, 4 * q : 4 * q + 4, :].bitcast(I32))
+        gi_c = load_by_place(gi, "gi_c")
         xw = sb([P, T], U32, "xw")
         nc.sync.dma_start(xw[:].bitcast(I32), x_words[0].rearrange("p n t -> p (n t)").bitcast(I32))
+        unread = sb([P, 1], F32, "unread")
+        nc.scalar.activation(unread[:], gi_c[:, 0:1], ACT.Sigmoid)
+        gt_c = load_by_place(gt, "gt_c")
+        for q in range(4):
+            nc.sync.dma_start(xs[32 * q : 32 * q + 4, :].bitcast(I32), x_scales[0, 4 * q : 4 * q + 4, :].bitcast(I32))
+        wb_rows = wb.rearrange("(p j) c -> p j c", j=PACK)
+        wb_raw = [sb([P, PACK, HALF], F32, f"wb_raw{h}") for h in range(2)]
+        for h in range(2):
+            nc.sync.dma_start(wb_raw[h][:], wb_rows[:, :, halves[h]])
         wa_raw = sb([P, PACK, H], F32, "wa_raw")
         nc.sync.dma_start(wa_raw[:], wa.rearrange("(p j) c -> p j c", j=PACK))
+        n2_l = load_list(n2, "n2_l")
+        n1_l = load_list(n1, "n1_l")
+        n3_l = load_list(n3, "n3_l")
         n4_l = load_list(n4, "n4_l")
 
-        def pick(window, lst, dtype, name, tag):
-            dst = keep.tile([P, S], dtype, name=name, tag=tag, align_bytes=64)
+        def pick(window, lst, dtype, name, buffer=""):
+            dst = sb([P, S], dtype, name, buffer)
             nc.vector.tensor_copy(dst[:].rearrange("p (t m) -> p m t", t=PACK), window[:].indirect(lst[:]))
             return dst
 
-        wb_woven = sb([P, H, PACK], BF16, "wb_woven")
+        xb_w = pick(xw, two_l, U32, "xb_w")
+        xb_s = pick(xs, two_l, U8, "xb_s")
         wb_q = sb([P, H], U32, "wb_q")
         wb_s = sb([P, H], U8, "wb_s")
-        nc.scalar.copy(weave_out(wb_woven[:, :HALF, :]), weave_in(wb_raw[:, :, :HALF]))
-        nc.scalar.copy(weave_out(wb_woven[:, HALF:, :]), weave_in(wb_raw[:, :, HALF:]))
-        xb_s = pick(xs, two_l, U8, "xb_s", "xb_s")
-        quantize(wb_q[:, :HALF], wb_s[:, :HALF], wb_woven[:, :HALF, :])
-        xb_w = pick(xw, two_l, U32, "xb_w", "xb_w")
-        quantize(wb_q[:, HALF:], wb_s[:, HALF:], wb_woven[:, HALF:, :])
-        xa_s = pick(xs, offs_l, U8, "xa_s", "xa_s")
-        xa_w = pick(xw, offs_l, U32, "xa_w", "xa_w")
+        for h in range(2):
+            wb_woven = sb([P, HALF, PACK], BF16, f"wb_woven{h}", f"wb_woven{h}")
+            nc.scalar.copy(weave_out(wb_woven[:]), weave_in(wb_raw[h][:]))
+            quantize(wb_q[:, halves[h]], wb_s[:, halves[h]], wb_woven[:])
+        xa_s = pick(xs, offs_l, U8, "xa_s", "wb_woven0")
+        xa_w = pick(xw, offs_l, U32, "xa_w", "wb_woven1")
+
+        def project(name, c, tag, x_w, x_s, w_q, w_s):
+            bank = psum.tile([P, PACK, BLK], F32, name=name, tag=tag)
+            for t in range(PACK):
+                places = slice(t * P, (t + 1) * P)
+                product(bank[:, t, :], x_w[:, places], x_s[:, places], w_q[:, blocks[c]], w_s[:, blocks[c]])
+            return bank
 
         sig_b = sb([P, PACK, H], F32, "sig_b")
         b_bank = []
         for c in range(NBLK):
-            bank = psum.tile([P, PACK, BLK], F32, name=f"b_bank{c}", tag=f"left{c}")
-            cols = slice(c * BLK, (c + 1) * BLK)
-            for t in range(PACK):
-                toks = slice(t * P, (t + 1) * P)
-                product(bank[:, t, :], xb_w[:, toks], xb_s[:, toks], wb_q[:, cols], wb_s[:, cols])
-            nc.scalar.activation(sig_b[:, :, c * BLK : (c + 1) * BLK], bank[:], ACT.Sigmoid)
-            b_bank.append(bank)
+            b_bank.append(project(f"b_bank{c}", c, f"left{c}", xb_w, xb_s, wb_q, wb_s))
+            nc.scalar.activation(sig_b[:, :, blocks[c]], b_bank[c][:], ACT.Sigmoid)
 
-        wa_woven = sb([P, H, PACK], BF16, "wa_woven")
+        wa_woven = sb([P, H, PACK], BF16, "wa_woven", "woven")
         wa_q = sb([P, H], U32, "wa_q")
         wa_s = sb([P, H], U8, "wa_s")
-        nc.vector.tensor_copy(weave_out(wa_woven[:]), weave_in(wa_raw[:]))
-        z2_woven = sb([P, H, PACK], BF16, "z2_woven")
-        gi_b = gi_c[:].unsqueeze(1).to_broadcast([P, BLK, PACK])
+        for cols in halves:
+            nc.vector.tensor_copy(weave_out(wa_woven[:, cols, :]), weave_in(wa_raw[:, :, cols]))
+        for cols in halves:
+            quantize(wa_q[:, cols], wa_s[:, cols], wa_woven[:, cols, :])
 
-        def make_z2(c):
-            nc.vector.tensor_tensor(z2_woven[:, c * BLK : (c + 1) * BLK, :], b_bank[c][:].rearrange("p t c -> p c t"), gi_b, ALU.mult)
+        def look_up(name, rows, lst, scale):
+            found = [sb([P, PACK, HALF], F32, f"{name}{h}") for h in range(2)]
+            for h in range(2):
+                entries = lst[:, h * HALF // 16 : (h + 1) * HALF // 16]
+                for t in range(PACK):
+                    nc.scalar.activation(found[h][:, t, :], rows[:, t, :].indirect(entries), ACT.Copy, scale=scale)
+            return found
 
-        quantize(wa_q[:], wa_s[:], wa_woven[:])
+        gate = look_up("gate", sig_b, n2_l, 1.0)
 
-        gate = sb([P, PACK, H], F32, "gate")
-        for h in range(2):
-            for t in range(PACK):
-                nc.scalar.activation(gate[:, t, h * HALF : (h + 1) * HALF], sig_b[:, t, :].indirect(entries(n2_l, h * HALF, HALF)), ACT.Copy)
-
-        half_a = sb([P, PACK, H], F32, "half_a")
-        half_gt = sb([P, PACK], F32, "half_gt")
-        nc.vector.tensor_scalar(half_gt[:], gt_c[:], 0.5, None, ALU.mult)
+        gt_a = sb([P, PACK, H], F32, "gt_a")
         for c in range(NBLK):
-            bank = psum.tile([P, PACK, BLK], F32, name=f"a_bank{c}", tag=f"right{c}")
-            cols = slice(c * BLK, (c + 1) * BLK)
-            for t in range(PACK):
-                toks = slice(t * P, (t + 1) * P)
-                product(bank[:, t, :], xa_w[:, toks], xa_s[:, toks], wa_q[:, cols], wa_s[:, cols])
-            nc.vector.tensor_tensor(half_a[:, :, cols], bank[:], half_gt[:].unsqueeze(2).to_broadcast([P, PACK, BLK]), ALU.mult)
-        for c in range(NBLK):
-            make_z2(c)
+            bank = project(f"a_bank{c}", c, f"right{c}", xa_w, xa_s, wa_q, wa_s)
+            nc.vector.tensor_tensor(gt_a[:, :, blocks[c]], bank[:], gt_c[:].unsqueeze(2).to_broadcast([P, PACK, BLK]), ALU.mult)
+
+        z2_woven = sb([P, H, PACK], BF16, "z2_woven", "woven")
         z2_q = sb([P, H], U32, "z2_q")
         z2_s = sb([P, H], U8, "z2_s")
 
-        looked = [sb([P, PACK, BLK], F32, f"looked{c}") for c in range(NBLK)]
-        for c in range(NBLK):
-            for t in range(PACK):
-                nc.scalar.activation(looked[c][:, t, :], half_a[:, t, :].indirect(entries(n1_l, c * BLK, BLK)), ACT.Copy)
+        def make_z2(c):
+            nc.vector.tensor_tensor(z2_woven[:, blocks[c], :], b_bank[c][:].rearrange("p t c -> p c t"),
+                                    gi_c[:].unsqueeze(1).to_broadcast([P, BLK, PACK]), ALU.mult)
 
-        cv = []
+        for c in range(NBLK - 1):
+            make_z2(c)
+        quantize(z2_q[:, halves[0]], z2_s[:, halves[0]], z2_woven[:, halves[0], :])
+        make_z2(NBLK - 1)
+        quantize(z2_q[:, halves[1]], z2_s[:, halves[1]], z2_woven[:, halves[1], :])
+
+        less = look_up("less", gt_a, n1_l, 0.5)
+
+        cv, ra = [], []
 
         def make_cv(c):
-            cols = slice(c * BLK, (c + 1) * BLK)
             gated = sb([P, PACK, BLK], F32, f"gated{c}")
-            nc.vector.scalar_tensor_tensor(gated[:], half_a[:, :, cols], 2.0, gate[:, :, cols], ALU.mult, ALU.mult)
-            if c == 0:
-                quantize(z2_q[:], z2_s[:], z2_woven[:])
+            engine = nc.gpsimd if c < GPSIMD_BLOCKS else nc.vector
+            engine.tensor_tensor(gated[:], gt_a[:, :, blocks[c]], in_half(gate, c), ALU.mult)
             z_woven = sb([P, BLK, PACK], BF16, f"z_woven{c}")
-            nc.vector.tensor_tensor(weave_out(z_woven[:]), weave_in(gated[:]), weave_in(looked[c][:]), ALU.subtract)
-            z_q = sb([P, BLK], U32, f"z_q{c}")
+            nc.vector.tensor_tensor(weave_out(z_woven[:]), weave_in(gated[:]), weave_in(in_half(less, c)), ALU.subtract)
+            z_q = sb([P, BLK], U32, f"z_q{c}", f"z_q{c}")
             z_s = sb([P, BLK], U8, f"z_s{c}")
             quantize(z_q[:], z_s[:], z_woven[:])
             bank = psum.tile([P, H], F32, name=f"cv_bank{c}", tag=f"left{c}")
@@ -157,24 +170,23 @@ def tile_picked_momtgatebfold_none_p_kernel(tc, x_words, x_scales, wa, wb, gt, g
             nc.vector.tensor_scalar(rows[:], bank[:], 0.0625, None, ALU.mult)
             cv.append(rows)
 
-        ra = []
-
         def fetch(c):
             pa = sb([P, W], F32, f"pa{c}")
-            pb = sb([P, W], F32, f"pb{c}")
+            sig_pb = sb([P, W], F32, f"sig_pb{c}")
             nc.scalar.activation(pa[:], cv[c][:].indirect(n3_l[:]), ACT.Copy)
-            nc.scalar.activation(pb[:], cv[c][:].indirect(n4_l[:]), ACT.Sigmoid)
-            r = sb([P, W], F32, f"ra{c}")
-            nc.vector.tensor_tensor(r[:], pa[:], pb[:], ALU.mult)
-            ra.append(r)
+            nc.scalar.activation(sig_pb[:], cv[c][:].indirect(n4_l[:]), ACT.Sigmoid)
+            rows = sb([P, W], F32, f"ra{c}", f"z_q{c + 1}")
+            nc.vector.tensor_tensor(rows[:], pa[:], sig_pb[:], ALU.mult)
+            ra.append(rows)
 
         def put(c):
             nc.scalar.activation(cv[c][:].indirect(n4_l[:]), ra[c][:], ACT.Copy)
-            nc.sync.dma_start(out[c * BLK : (c + 1) * BLK, :], cv[c][:])
+            nc.sync.dma_start(out[blocks[c], :], cv[c][:])
 
+        make_cv(0)
         for c in range(NBLK):
-            make_cv(c)
-        for c in range(NBLK):
+            if c + 1 < NBLK:
+                make_cv(c + 1)
             fetch(c)
             if c > 0:
                 put(c - 1)

from contextlib import ExitStack

import concourse.mybir as mybir

T, S, H, W = 2048, 512, 512, 256
FLOPS = 3 * 2 * 512 * 512 * 512

F32 = mybir.dt.float32
BF16 = mybir.dt.bfloat16
U32 = mybir.dt.uint32
I32 = mybir.dt.int32
U16 = mybir.dt.uint16
U8 = mybir.dt.uint8
FP8X4 = mybir.dt.float8_e4m3fn_x4
ACT = mybir.ActivationFunctionType
ALU = mybir.AluOpType

P = 128
PACK = 4
BLK = 128
NBLK = H // BLK
HALF = H // 2
LINE = 4
GPSIMD_BLOCKS = NBLK - 1


def tile_picked_momtgatebfold_none_p_kernel(tc, x_words, x_scales, wa, wb, gt, gi, offs, two, n1, n2, n3, n4, out):
    nc = tc.nc
    with ExitStack() as ctx:
        keep = ctx.enter_context(tc.tile_pool(name="keep", bufs=1))
        psum = ctx.enter_context(tc.psum_pool(name="psum", bufs=1))

        def sb(shape, dtype, name, buffer=""):
            return keep.tile(shape, dtype, name=name, tag=buffer, align_bytes=64)

        def load_list(src, name):
            dst = keep.tile(list(src.shape), U16, name=name)
            nc.sync.dma_start(dst[:], src)
            return dst

        def load_by_place(src, name):
            dst = sb([P, PACK], F32, name)
            nc.sync.dma_start(dst[:], src.rearrange("(p t) o -> p (t o)", t=PACK))
            return dst

        def weave_out(woven):
            return woven.rearrange("p (c i) t -> p c t i", i=LINE)

        def weave_in(rows):
            return rows.rearrange("p t (c i) -> p c t i", i=LINE)

        def quantize(codes, scales, woven):
            nc.vector.quantize_mx(out=codes.bitcast(FP8X4), scales=scales, in_=woven.rearrange("p c t -> p (c t)"))

        def product(acc, l_codes, l_scales, r_codes, r_scales):
            nc.tensor.matmul_mx(out=acc, lhsT=l_codes.bitcast(FP8X4), lhsT_scale=l_scales,
                                rhs=r_codes.bitcast(FP8X4), rhs_scale=r_scales, start=True, stop=True)

        blocks = [slice(c * BLK, (c + 1) * BLK) for c in range(NBLK)]
        halves = [slice(h * HALF, (h + 1) * HALF) for h in range(2)]

        def in_half(tiles, c):
            return tiles[c // 2][:, :, blocks[c % 2]]

        xs = sb([P, T], U8, "xs")
        nc.vector.memset(xs[:].bitcast(I32), 0)
        two_l = load_list(two, "two_l")
        offs_l = load_list(offs, "offs_l")
        gi_c = load_by_place(gi, "gi_c")
        xw = sb([P, T], U32, "xw")
        nc.sync.dma_start(xw[:].bitcast(I32), x_words[0].rearrange("p n t -> p (n t)").bitcast(I32))
        unread = sb([P, 1], F32, "unread")
        nc.scalar.activation(unread[:], gi_c[:, 0:1], ACT.Sigmoid)
        gt_c = load_by_place(gt, "gt_c")
        for q in range(4):
            nc.sync.dma_start(xs[32 * q : 32 * q + 4, :].bitcast(I32), x_scales[0, 4 * q : 4 * q + 4, :].bitcast(I32))
        wb_rows = wb.rearrange("(p j) c -> p j c", j=PACK)
        wb_raw = [sb([P, PACK, HALF], F32, f"wb_raw{h}") for h in range(2)]
        for h in range(2):
            nc.sync.dma_start(wb_raw[h][:], wb_rows[:, :, halves[h]])
        wa_raw = sb([P, PACK, H], F32, "wa_raw")
        nc.sync.dma_start(wa_raw[:], wa.rearrange("(p j) c -> p j c", j=PACK))
        n2_l = load_list(n2, "n2_l")
        n1_l = load_list(n1, "n1_l")
        n3_l = load_list(n3, "n3_l")
        n4_l = load_list(n4, "n4_l")

        def pick(window, lst, dtype, name, buffer=""):
            dst = sb([P, S], dtype, name, buffer)
            nc.vector.tensor_copy(dst[:].rearrange("p (t m) -> p m t", t=PACK), window[:].indirect(lst[:]))
            return dst

        xb_w = pick(xw, two_l, U32, "xb_w")
        xb_s = pick(xs, two_l, U8, "xb_s")
        wb_q = sb([P, H], U32, "wb_q")
        wb_s = sb([P, H], U8, "wb_s")
        for h in range(2):
            wb_woven = sb([P, HALF, PACK], BF16, f"wb_woven{h}", f"wb_woven{h}")
            nc.scalar.copy(weave_out(wb_woven[:]), weave_in(wb_raw[h][:]))
            quantize(wb_q[:, halves[h]], wb_s[:, halves[h]], wb_woven[:])
        xa_s = pick(xs, offs_l, U8, "xa_s", "wb_woven0")
        xa_w = pick(xw, offs_l, U32, "xa_w", "wb_woven1")

        def project(name, c, tag, x_w, x_s, w_q, w_s):
            bank = psum.tile([P, PACK, BLK], F32, name=name, tag=tag)
            for t in range(PACK):
                places = slice(t * P, (t + 1) * P)
                product(bank[:, t, :], x_w[:, places], x_s[:, places], w_q[:, blocks[c]], w_s[:, blocks[c]])
            return bank

        sig_b = sb([P, PACK, H], F32, "sig_b")
        b_bank = []
        for c in range(NBLK):
            b_bank.append(project(f"b_bank{c}", c, f"left{c}", xb_w, xb_s, wb_q, wb_s))
            nc.scalar.activation(sig_b[:, :, blocks[c]], b_bank[c][:], ACT.Sigmoid)

        wa_woven = sb([P, H, PACK], BF16, "wa_woven", "woven")
        wa_q = sb([P, H], U32, "wa_q")
        wa_s = sb([P, H], U8, "wa_s")
        for cols in halves:
            nc.vector.tensor_copy(weave_out(wa_woven[:, cols, :]), weave_in(wa_raw[:, :, cols]))
        for cols in halves:
            quantize(wa_q[:, cols], wa_s[:, cols], wa_woven[:, cols, :])

        def look_up(name, rows, lst, scale):
            found = [sb([P, PACK, HALF], F32, f"{name}{h}") for h in range(2)]
            for h in range(2):
                entries = lst[:, h * HALF // 16 : (h + 1) * HALF // 16]
                for t in range(PACK):
                    nc.scalar.activation(found[h][:, t, :], rows[:, t, :].indirect(entries), ACT.Copy, scale=scale)
            return found

        gate = look_up("gate", sig_b, n2_l, 1.0)

        gt_a = sb([P, PACK, H], F32, "gt_a")
        for c in range(NBLK):
            bank = project(f"a_bank{c}", c, f"right{c}", xa_w, xa_s, wa_q, wa_s)
            nc.vector.tensor_tensor(gt_a[:, :, blocks[c]], bank[:], gt_c[:].unsqueeze(2).to_broadcast([P, PACK, BLK]), ALU.mult)

        z2_woven = sb([P, H, PACK], BF16, "z2_woven", "woven")
        z2_q = sb([P, H], U32, "z2_q")
        z2_s = sb([P, H], U8, "z2_s")

        def make_z2(c):
            nc.vector.tensor_tensor(z2_woven[:, blocks[c], :], b_bank[c][:].rearrange("p t c -> p c t"),
                                    gi_c[:].unsqueeze(1).to_broadcast([P, BLK, PACK]), ALU.mult)

        for c in range(NBLK - 1):
            make_z2(c)
        quantize(z2_q[:, halves[0]], z2_s[:, halves[0]], z2_woven[:, halves[0], :])
        make_z2(NBLK - 1)
        quantize(z2_q[:, halves[1]], z2_s[:, halves[1]], z2_woven[:, halves[1], :])

        less = look_up("less", gt_a, n1_l, 0.5)

        cv, ra = [], []

        def make_cv(c):
            gated = sb([P, PACK, BLK], F32, f"gated{c}")
            engine = nc.gpsimd if c < GPSIMD_BLOCKS else nc.vector
            engine.tensor_tensor(gated[:], gt_a[:, :, blocks[c]], in_half(gate, c), ALU.mult)
            z_woven = sb([P, BLK, PACK], BF16, f"z_woven{c}")
            nc.vector.tensor_tensor(weave_out(z_woven[:]), weave_in(gated[:]), weave_in(in_half(less, c)), ALU.subtract)
            z_q = sb([P, BLK], U32, f"z_q{c}", f"z_q{c}")
            z_s = sb([P, BLK], U8, f"z_s{c}")
            quantize(z_q[:], z_s[:], z_woven[:])
            bank = psum.tile([P, H], F32, name=f"cv_bank{c}", tag=f"left{c}")
            product(bank[:], z_q[:], z_s[:], z2_q[:], z2_s[:])
            rows = sb([P, H], F32, f"cv{c}")
            nc.vector.tensor_scalar(rows[:], bank[:], 0.0625, None, ALU.mult)
            cv.append(rows)

        def fetch(c):
            pa = sb([P, W], F32, f"pa{c}")
            sig_pb = sb([P, W], F32, f"sig_pb{c}")
            nc.scalar.activation(pa[:], cv[c][:].indirect(n3_l[:]), ACT.Copy)
            nc.scalar.activation(sig_pb[:], cv[c][:].indirect(n4_l[:]), ACT.Sigmoid)
            rows = sb([P, W], F32, f"ra{c}", f"z_q{c + 1}")
            nc.vector.tensor_tensor(rows[:], pa[:], sig_pb[:], ALU.mult)
            ra.append(rows)

        def put(c):
            nc.scalar.activation(cv[c][:].indirect(n4_l[:]), ra[c][:], ACT.Copy)
            nc.sync.dma_start(out[blocks[c], :], cv[c][:])

        make_cv(0)
        for c in range(NBLK):
            if c + 1 < NBLK:
                make_cv(c + 1)
            fetch(c)
            if c > 0:
                put(c - 1)
        put(NBLK - 1)
